import numpy as np
import ml_dtypes


def mxq(x, axis, fmt="e4m3"):
    dtype, down = {"e4m3": (ml_dtypes.float8_e4m3fn, 7), "e5m2": (ml_dtypes.float8_e5m2, 14)}[fmt]
    v = np.moveaxis(np.asarray(x, np.float32).astype(ml_dtypes.bfloat16).astype(np.float64), axis, -1)
    blocks = v.reshape(v.shape[:-1] + (-1, 32))
    amax = np.abs(blocks).max(-1, keepdims=True)
    byte = np.maximum(np.where(amax > 0, np.frexp(amax)[1] - 1 + 127, 0) - down, 1)
    scale = np.exp2(byte - 127.0)
    codes = (blocks / scale).astype(np.float32).astype(dtype).astype(np.float64)
    return np.moveaxis((codes * scale).reshape(v.shape), -1, axis)


WIDE = False


def mx_kscale(k):
    if not WIDE:
        return np.ones(k)
    levels = np.array([10, -10, 5, -5, 0])
    if k % 512:
        return np.exp2(np.random.permutation(np.resize(levels, k // 32))).repeat(32)
    a = np.empty((k // 512, 16))
    for p in range(k // 512):
        a[p, :8] = np.random.permutation(np.resize(levels, 8))
        for g in range(8):
            far = levels[np.abs(levels - a[p, g]) >= 10]
            a[p, g + 8] = far[np.random.randint(len(far))]
    return np.exp2(a.ravel()).repeat(32)


def f64(x):
    return np.asarray(x).astype(np.float64)


def striped(idx):
    return np.tile(idx.reshape(-1, 16).T, (8, 1)).astype(np.uint16)


def unstriped(offs):
    return offs[:16].T.reshape(-1).astype(np.int64)


def pack_weight(w):
    k, n = w.shape
    w = f64(np.asarray(w, np.float32).astype(ml_dtypes.bfloat16)).reshape(k // 32, 32, n)
    amax = np.abs(w).max(1)
    byte = np.clip(np.where(amax > 0, np.frexp(amax)[1] - 1 + 127 - 7, 1), 1, 254)
    scaled = (w * np.exp2(127.0 - byte)[:, None, :]).reshape(k, n).astype(np.float32)
    words = np.ascontiguousarray(scaled.reshape(k // 512, 128, 4, n).transpose(0, 1, 3, 2)).astype(ml_dtypes.float8_e4m3fn).view(np.uint8)
    return words, np.ascontiguousarray(byte.astype(np.uint8).reshape(k // 512, 16, n))


def unpack_weight(words, scales):
    g, p, n, _ = words.shape
    vals = np.ascontiguousarray(words).view(ml_dtypes.float8_e4m3fn).astype(np.float64) * np.repeat(np.exp2(scales.astype(np.float64) - 127.0), 8, axis=1)[..., None]
    return vals.transpose(0, 1, 3, 2).reshape(g * 512, n)


def gelu(v):
    return 0.5 * v * (1.0 + np.tanh(np.sqrt(2.0 / np.pi) * (v + 0.044715 * v**3)))


K, T, S, J, H, N = 512, 4096, 1024, 512, 512, 128


def setup_inputs():
    n = np.random.standard_normal
    s = mx_kscale(K)[:, None]
    u = mx_kscale(H)
    r = mx_kscale(J)[:, None]
    packed = pack_weight(n((K, T)) * s)
    return {
        "x_words": packed[0],
        "x_scales": packed[1],
        "eT": (n((J, S)) * r).astype(np.float32),
        "w1": (n((K, H)) / np.sqrt(K) / s * u).astype(np.float32),
        "w3": (n((J, H)) / np.sqrt(J) / r).astype(np.float32),
        "w2": (n((H, N)) / np.sqrt(H) / u[:, None]).astype(np.float32),
        "offs": striped(np.random.permutation(T)[:S]),
    }


def reference(x_words, x_scales, eT, w1, w3, w2, offs):
    c = mxq(f64(w1), 0, "e4m3").T @ unpack_weight(x_words, x_scales)[:, unstriped(offs)]
    z = c * gelu(mxq(f64(w3), 0, "e4m3").T @ mxq(f64(eT), 0, "e4m3"))
    return mxq(f64(w2), 0, "e4m3").T @ mxq(z, 0, "e4m3")

@@ -1,0 +1,239 @@
+from contextlib import ExitStack
+
+import concourse.mybir as mybir
+
+K, T, S, J, H, N = 512, 4096, 1024, 512, 512, 128
+FLOPS = 2 * S * (K * H + J * H + H * N)
+
+F32 = mybir.dt.float32
+BF16 = mybir.dt.bfloat16
+I32 = mybir.dt.int32
+U32 = mybir.dt.uint32
+U16 = mybir.dt.uint16
+U8 = mybir.dt.uint8
+FP8X4 = mybir.dt.float8_e4m3fn_x4
+GELU = mybir.ActivationFunctionType.Gelu_apprx_tanh
+MULT = mybir.AluOpType.mult
+
+P = 128
+PACK = 4
+CHUNK = 128
+CHUNKS = S // CHUNK
+PIECES = (2, 2, 2, 2)
+LEAD_CAST, LEAD_QUANT, LEAD_FILTER, LAG = 4, 3, 2, 1
+GATHER = 512
+HALF = H // 2
+OUT_GROUPS = ((0, 1), (2, 3), (4, 5), (6,), (7,))
+E_GROUPS = (((0,), "scalar"), ((1,), "scalar"), ((2,), "vector"), ((3,), "scalar"), ((4,), "scalar"), ((5,), "scalar"), ((6,), "vector"), ((7,), "scalar"))
+
+
+def tile_picked_schnet_gelu_p_kernel(tc, x_words, x_scales, eT, w1, w3, w2, offs, out):
+    nc = tc.nc
+    with ExitStack() as ctx:
+        keep = ctx.enter_context(tc.tile_pool(name="keep", bufs=1))
+        psum = ctx.enter_context(tc.psum_pool(name="psum", bufs=1))
+
+        def sb(name, shape, dtype, slot=None):
+            return keep.tile(shape, dtype, name=name, tag=slot or name, align_bytes=64)
+
+        def copy_on(engine, dst, src):
+            if engine == "vector":
+                nc.vector.tensor_copy(out=dst, in_=src)
+            else:
+                nc.scalar.copy(out=dst, in_=src)
+
+        def quantize(codes, scales, values):
+            nc.vector.quantize_mx(out=codes.bitcast(FP8X4), scales=scales, in_=values)
+
+        def mx(acc, lhs, lhs_cols, rhs, rhs_cols):
+            nc.tensor.matmul_mx(
+                out=acc,
+                lhsT=lhs[0][:, lhs_cols].bitcast(FP8X4),
+                lhsT_scale=lhs[1][:, lhs_cols],
+                rhs=rhs[0][:, rhs_cols].bitcast(FP8X4),
+                rhs_scale=rhs[1][:, rhs_cols],
+                start=True,
+                stop=True,
+            )
+
+        def load_rows(name, src, cols, slot):
+            raw = sb(name, [P, PACK, cols.stop - cols.start], F32, slot)
+            nc.sync.dma_start(out=raw[:], in_=src.rearrange("(p j) c -> p j c", j=PACK)[:, :, cols])
+            return raw
+
+        def mx_tiles(name, width):
+            return sb(name + "_codes", [P, width], U32), sb(name + "_scales", [P, width], U8)
+
+        def deal(engine, dealt, raw, h, t0, tn):
+            ms = HALF // PACK
+            copy_on(
+                engine,
+                dealt[:].rearrange("p (t m j) -> p m j t", t=tn, j=PACK)[:, h * ms : (h + 1) * ms, :, :],
+                raw[:].rearrange("p j (m t) -> p m j t", t=PACK)[:, :, :, t0 : t0 + tn],
+            )
+
+        def weave(name, engine, raw_cols, slot=None):
+            width = raw_cols.shape[2]
+            woven = sb(name, [P, width * PACK], BF16, slot)
+            copy_on(
+                engine,
+                woven[:].rearrange("p (c i j) -> p c j i", i=4, j=PACK),
+                raw_cols.rearrange("p j (c i) -> p c j i", i=4),
+            )
+            return woven
+
+        def half_cols(h):
+            return slice(h * HALF, (h + 1) * HALF)
+
+        def piece_cols(i):
+            return slice(sum(PIECES[:i]) * CHUNK, sum(PIECES[: i + 1]) * CHUNK)
+
+        table_scales = sb("table_scales", [P, T], U8, "scale_table")
+        nc.vector.memset(table_scales[:].bitcast(I32), 0)
+        zero_in = sb("zero_in", [P, 1], F32, "table")
+        nc.vector.memset(zero_in[:], 0.0)
+        zero_bias = sb("zero_bias", [P, 1], F32)
+        nc.scalar.activation(out=zero_bias[:], in_=zero_in[:], func=GELU)
+
+        w3_raw = [load_rows("w3_raw%d" % h, w3, half_cols(h), "w_stage%d" % h) for h in range(2)]
+        offsets = keep.tile([P, S // 16], U16, name="offsets")
+        nc.sync.dma_start(offsets[:], offs)
+        e_raw = [load_rows("e_raw0", eT, piece_cols(0), "e_stage")]
+        for r in range(4):
+            nc.sync.dma_start(out=table_scales[r:P:32, :].bitcast(I32), in_=x_scales[0, r:16:4, :].bitcast(I32))
+        table_words = sb("table_words", [P, T], U32, "table")
+        nc.sync.dma_start(out=table_words[:].bitcast(I32), in_=x_words[0].rearrange("p c r -> p (c r)").bitcast(I32))
+
+        w3_mx = mx_tiles("w3", H)
+        w3_dealt = sb("w3_dealt", [P, H * PACK], BF16)
+        for h in range(2):
+            deal("vector", w3_dealt, w3_raw[h], h, 0, PACK)
+        quantize(w3_mx[0][:], w3_mx[1][:], w3_dealt[:])
+        w1_raw = [load_rows("w1_raw%d" % h, w1, half_cols(h), "w_stage%d" % h) for h in range(2)]
+        e_raw.append(load_rows("e_raw1", eT, piece_cols(1), "w3_dealt"))
+
+        e_mx = {}
+        gate = {}
+        c_acc = {}
+        z_tiles = {}
+        z_mx = {}
+        group_of = {c: g for g in OUT_GROUPS for c in g}
+
+        e_woven = {}
+
+        e_group_at = {g[0]: (g, engine) for g, engine in E_GROUPS}
+
+        def cast_e(c):
+            if c in e_group_at:
+                g, engine = e_group_at[c]
+                piece = max(i for i in range(len(PIECES)) if sum(PIECES[:i]) <= c)
+                at = (c - sum(PIECES[:piece])) * CHUNK
+                e_woven[c] = weave("e_woven%d" % c, engine, e_raw[piece][:, :, at : at + len(g) * CHUNK])
+
+        def quantize_e(c):
+            if c in e_group_at:
+                g = e_group_at[c][0]
+                tiles = mx_tiles("e%d" % c, len(g) * CHUNK)
+                quantize(tiles[0][:], tiles[1][:], e_woven[c][:])
+                for member in g:
+                    e_mx[member] = (tiles, (member - c) * CHUNK)
+
+        def filter_of(c):
+            acc = psum.tile([P, PACK, CHUNK], F32, name="f_acc", tag="f_acc", bufs=3)
+            tiles, at = e_mx[c]
+            for t in range(PACK):
+                mx(acc[:, t, :], w3_mx, slice(t * P, (t + 1) * P), tiles, slice(at, at + CHUNK))
+            gate[c] = sb("gate%d" % c, [P, CHUNK * PACK], F32)
+            nc.scalar.activation(
+                out=gate[c][:].rearrange("p (n t) -> p n t", t=PACK),
+                in_=acc[:].rearrange("p t n -> p n t"),
+                func=GELU,
+                bias=zero_bias[:],
+            )
+
+        def atoms_of(c):
+            acc = psum.tile([P, PACK, CHUNK], F32, name="c_acc", tag="c_acc", bufs=3)
+            half, at = divmod(c * CHUNK, GATHER)
+            for t in range(PACK):
+                nc.tensor.matmul_mx(
+                    out=acc[:, t, :],
+                    lhsT=w1_mx[0][:, t * P : (t + 1) * P].bitcast(FP8X4),
+                    lhsT_scale=w1_mx[1][:, t * P : (t + 1) * P],
+                    rhs=picked_words[half][:, at : at + CHUNK].bitcast(FP8X4),
+                    rhs_scale=picked_scales[:, c * CHUNK : (c + 1) * CHUNK],
+                    start=True,
+                    stop=True,
+                )
+            c_acc[c] = acc
+
+        def message(c):
+            g = group_of[c]
+            if g not in z_tiles:
+                z_tiles[g] = sb("z%d" % c, [P, len(g) * CHUNK * PACK], BF16)
+            at = (c - g[0]) * CHUNK * PACK
+            nc.vector.tensor_tensor(
+                out=z_tiles[g][:, at : at + CHUNK * PACK].rearrange("p (n t) -> p n t", t=PACK),
+                in0=c_acc[c][:].rearrange("p t n -> p n t"),
+                in1=gate[c][:].rearrange("p (n t) -> p n t", t=PACK),
+                op=MULT,
+            )
+
+        def project(g):
+            width = len(g) * CHUNK
+            z_mx[g] = mx_tiles("z%d" % g[0], width)
+            quantize(z_mx[g][0][:], z_mx[g][1][:], z_tiles[g][:])
+            acc = psum.tile([P, 2 * CHUNK], F32, name="o_acc", tag="o_acc", bufs=2)
+            mx(acc[:, 0:width], w2_mx, slice(0, N), z_mx[g], slice(0, width))
+            res = sb("res%d" % g[0], [P, width], F32)
+            nc.scalar.copy(out=res[:], in_=acc[:, 0:width])
+            nc.sync.dma_start(out=out[:, g[0] * CHUNK : g[0] * CHUNK + width], in_=res[:])
+
+        for c in range(PIECES[0]):
+            cast_e(c)
+        for c in range(PIECES[0]):
+            quantize_e(c)
+        e_raw.append(load_rows("e_raw2", eT, piece_cols(2), "e_stage"))
+        e_raw.append(load_rows("e_raw3", eT, piece_cols(3), "e_woven1"))
+        for c in range(PIECES[0]):
+            filter_of(c)
+
+        picked_scales = sb("picked_scales", [P, S], U8)
+        nc.vector.tensor_copy(picked_scales[:], table_scales[:].indirect(offsets[:]))
+        w2_raw = load_rows("w2_raw", w2, slice(0, N), "scale_table")
+        picked_words = []
+        for h in range(S // GATHER):
+            words = sb("picked_words%d" % h, [P, GATHER], U32)
+            nc.vector.tensor_copy(words[:], table_words[:].indirect(offsets[:, h * GATHER // 16 : (h + 1) * GATHER // 16]))
+            picked_words.append(words)
+
+        w1_mx = mx_tiles("w1", H)
+        w1_dealt = [sb("w1_dealt%d" % u, [P, 2 * P * PACK], BF16) for u in range(2)]
+        for h in range(2):
+            for u in range(2):
+                deal("vector" if (h, u) == (1, 0) else "scalar", w1_dealt[u], w1_raw[h], h, 2 * u, 2)
+        for t in range(PACK):
+            cols = slice(t * P, (t + 1) * P)
+            at = (t % 2) * P * PACK
+            quantize(w1_mx[0][:, cols], w1_mx[1][:, cols], w1_dealt[t // 2][:, at : at + P * PACK])
+
+        w2_mx = mx_tiles("w2", N)
+
+        first = PIECES[0]
+        for step in range(-max(LEAD_CAST, LEAD_QUANT, LEAD_FILTER), CHUNKS + LAG):
+            if 0 <= step + 1 < CHUNKS:
+                atoms_of(step + 1)
+            if first <= step + LEAD_CAST < CHUNKS:
+                cast_e(step + LEAD_CAST)
+            if first <= step + LEAD_QUANT < CHUNKS:
+                quantize_e(step + LEAD_QUANT)
+            if first <= step + LEAD_FILTER < CHUNKS:
+                filter_of(step + LEAD_FILTER)
+            if 0 <= step < CHUNKS:
+                message(step)
+            if step == 0:
+                w2_woven = weave("w2_woven", "scalar", w2_raw[:])
+            if step == 1:
+                quantize(w2_mx[0][:], w2_mx[1][:], w2_woven[:])
+            done = step - LAG
+            if 0 <= done and group_of[done][-1] == done:
+                project(group_of[done])

@@ -22,6 +22,7 @@ CHUNKS = S // CHUNK
 PIECES = (2, 2, 2, 2)
 LEAD_CAST, LEAD_QUANT, LEAD_FILTER, LAG = 4, 3, 2, 1
 GATHER = 512
+W2_AFTER = 1
 HALF = H // 2
 OUT_GROUPS = ((0, 1), (2, 3), (4, 5), (6,), (7,))
 E_GROUPS = (((0,), "scalar"), ((1,), "scalar"), ((2,), "vector"), ((3,), "scalar"), ((4,), "scalar"), ((5,), "scalar"), ((6,), "vector"), ((7,), "scalar"))
@@ -56,21 +57,31 @@ def tile_picked_schnet_gelu_p_kernel(tc, x_words, x_scales, eT, w1, w3, w2, offs
                 stop=True,
             )
 
-        def load_rows(name, src, cols, slot):
-            raw = sb(name, [P, PACK, cols.stop - cols.start], F32, slot)
-            nc.sync.dma_start(out=raw[:], in_=src.rearrange("(p j) c -> p j c", j=PACK)[:, :, cols])
+        def load_into(flat, src, cols):
+            raw = flat.rearrange("p (j c) -> p j c", j=PACK)
+            nc.sync.dma_start(out=raw, in_=src.rearrange("(p j) c -> p j c", j=PACK)[:, :, cols])
             return raw
+
+        def load_rows(name, src, cols, slot):
+            flat = sb(name, [P, PACK * (cols.stop - cols.start)], F32, slot)
+            return load_into(flat[:], src, cols)
 
         def mx_tiles(name, width):
             return sb(name + "_codes", [P, width], U32), sb(name + "_scales", [P, width], U8)
 
-        def deal(engine, dealt, raw, h, t0, tn):
-            ms = HALF // PACK
+        def deal(engine, dealt, raw, m0, u):
+            ms = raw.shape[2] // PACK
             copy_on(
                 engine,
-                dealt[:].rearrange("p (t m j) -> p m j t", t=tn, j=PACK)[:, h * ms : (h + 1) * ms, :, :],
-                raw[:].rearrange("p j (m t) -> p m j t", t=PACK)[:, :, :, t0 : t0 + tn],
+                dealt[:].rearrange("p (t m j) -> p m j t", t=2, j=PACK)[:, m0 : m0 + ms, :, :],
+                raw.rearrange("p j (m t) -> p m j t", t=PACK)[:, :, :, 2 * u : 2 * u + 2],
             )
+
+        def quantize_dealt(w_mx, dealt):
+            for t in range(PACK):
+                cols = slice(t * P, (t + 1) * P)
+                at = (t % 2) * P * PACK
+                quantize(w_mx[0][:, cols], w_mx[1][:, cols], dealt[t // 2][:, at : at + P * PACK])
 
         def weave(name, engine, raw_cols, slot=None):
             width = raw_cols.shape[2]
@@ -95,22 +106,24 @@ def tile_picked_schnet_gelu_p_kernel(tc, x_words, x_scales, eT, w1, w3, w2, offs
         zero_bias = sb("zero_bias", [P, 1], F32)
         nc.scalar.activation(out=zero_bias[:], in_=zero_in[:], func=GELU)
 
-        w3_raw = [load_rows("w3_raw%d" % h, w3, half_cols(h), "w_stage%d" % h) for h in range(2)]
+        w3_raw = load_rows("w3_raw", w3, slice(0, H), "w_stage")
         offsets = keep.tile([P, S // 16], U16, name="offsets")
         nc.sync.dma_start(offsets[:], offs)
         e_raw = [load_rows("e_raw0", eT, piece_cols(0), "e_stage")]
-        for r in range(4):
-            nc.sync.dma_start(out=table_scales[r:P:32, :].bitcast(I32), in_=x_scales[0, r:16:4, :].bitcast(I32))
+        nc.sync.dma_start(out=table_scales[0:P:8, :].bitcast(I32), in_=x_scales[0].bitcast(I32))
         table_words = sb("table_words", [P, T], U32, "table")
         nc.sync.dma_start(out=table_words[:].bitcast(I32), in_=x_words[0].rearrange("p c r -> p (c r)").bitcast(I32))
+        placed_scales = sb("placed_scales", [P, S], U8)
+        nc.vector.memset(placed_scales[:].bitcast(I32), 0)
 
         w3_mx = mx_tiles("w3", H)
-        w3_dealt = sb("w3_dealt", [P, H * PACK], BF16)
-        for h in range(2):
-            deal("vector", w3_dealt, w3_raw[h], h, 0, PACK)
-        quantize(w3_mx[0][:], w3_mx[1][:], w3_dealt[:])
-        w1_raw = [load_rows("w1_raw%d" % h, w1, half_cols(h), "w_stage%d" % h) for h in range(2)]
-        e_raw.append(load_rows("e_raw1", eT, piece_cols(1), "w3_dealt"))
+        w3_dealt = [sb("w3_dealt%d" % u, [P, 2 * P * PACK], BF16) for u in range(2)]
+        deal("vector", w3_dealt[0], w3_raw, 0, 0)
+        deal("scalar", w3_dealt[1], w3_raw, 0, 1)
+        for u in range(2):
+            cols = slice(2 * u * P, 2 * (u + 1) * P)
+            quantize(w3_mx[0][:, cols], w3_mx[1][:, cols], w3_dealt[u][:])
+        w1_raw = [load_rows("w1_raw0", w1, half_cols(0), "w_stage"), load_rows("w1_raw1", w1, half_cols(1), "w3_dealt1")]
 
         e_mx = {}
         gate = {}
@@ -160,7 +173,7 @@ def tile_picked_schnet_gelu_p_kernel(tc, x_words, x_scales, eT, w1, w3, w2, offs
                     lhsT=w1_mx[0][:, t * P : (t + 1) * P].bitcast(FP8X4),
                     lhsT_scale=w1_mx[1][:, t * P : (t + 1) * P],
                     rhs=picked_words[half][:, at : at + CHUNK].bitcast(FP8X4),
-                    rhs_scale=picked_scales[:, c * CHUNK : (c + 1) * CHUNK],
+                    rhs_scale=placed_scales[:, c * CHUNK : (c + 1) * CHUNK],
                     start=True,
                     stop=True,
                 )
@@ -186,20 +199,28 @@ def tile_picked_schnet_gelu_p_kernel(tc, x_words, x_scales, eT, w1, w3, w2, offs
             mx(acc[:, 0:width], w2_mx, slice(0, N), z_mx[g], slice(0, width))
             res = sb("res%d" % g[0], [P, width], F32)
             nc.scalar.copy(out=res[:], in_=acc[:, 0:width])
-            nc.sync.dma_start(out=out[:, g[0] * CHUNK : g[0] * CHUNK + width], in_=res[:])
+            queue = nc.scalar if g == OUT_GROUPS[-1] else nc.sync
+            queue.dma_start(out=out[:, g[0] * CHUNK : g[0] * CHUNK + width], in_=res[:])
 
         for c in range(PIECES[0]):
             cast_e(c)
         for c in range(PIECES[0]):
             quantize_e(c)
-        e_raw.append(load_rows("e_raw2", eT, piece_cols(2), "e_stage"))
-        e_raw.append(load_rows("e_raw3", eT, piece_cols(3), "e_woven1"))
         for c in range(PIECES[0]):
             filter_of(c)
 
         picked_scales = sb("picked_scales", [P, S], U8)
         nc.vector.tensor_copy(picked_scales[:], table_scales[:].indirect(offsets[:]))
-        w2_raw = load_rows("w2_raw", w2, slice(0, N), "scale_table")
+        for r in range(4):
+            nc.sync.dma_start(out=placed_scales[r:P:32, :].bitcast(I32), in_=picked_scales[8 * r : P : 32, :].bitcast(I32))
+        late = sb("late", [P, PACK * (S - PIECES[0] * CHUNK + N)], F32, "scale_table")
+        at = 0
+        for i in range(1, len(PIECES)):
+            e_raw.append(load_into(late[:, at : at + PACK * PIECES[i] * CHUNK], eT, piece_cols(i)))
+            at = at + PACK * PIECES[i] * CHUNK
+            if i == W2_AFTER:
+                w2_raw = load_into(late[:, at : at + PACK * N], w2, slice(0, N))
+                at = at + PACK * N
         picked_words = []
         for h in range(S // GATHER):
             words = sb("picked_words%d" % h, [P, GATHER], U32)
@@ -210,11 +231,8 @@ def tile_picked_schnet_gelu_p_kernel(tc, x_words, x_scales, eT, w1, w3, w2, offs
         w1_dealt = [sb("w1_dealt%d" % u, [P, 2 * P * PACK], BF16) for u in range(2)]
         for h in range(2):
             for u in range(2):
-                deal("vector" if (h, u) == (1, 0) else "scalar", w1_dealt[u], w1_raw[h], h, 2 * u, 2)
-        for t in range(PACK):
-            cols = slice(t * P, (t + 1) * P)
-            at = (t % 2) * P * PACK
-            quantize(w1_mx[0][:, cols], w1_mx[1][:, cols], w1_dealt[t // 2][:, at : at + P * PACK])
+                deal("vector" if (h, u) == (1, 0) else "scalar", w1_dealt[u], w1_raw[h], h * HALF // PACK, u)
+        quantize_dealt(w1_mx, w1_dealt)
 
         w2_mx = mx_tiles("w2", N)
 
@@ -231,7 +249,7 @@ def tile_picked_schnet_gelu_p_kernel(tc, x_words, x_scales, eT, w1, w3, w2, offs
             if 0 <= step < CHUNKS:
                 message(step)
             if step == 0:
-                w2_woven = weave("w2_woven", "scalar", w2_raw[:])
+                w2_woven = weave("w2_woven", "scalar", w2_raw)
             if step == 1:
                 quantize(w2_mx[0][:], w2_mx[1][:], w2_woven[:])
             done = step - LAG

@@ -22,7 +22,8 @@ CHUNKS = S // CHUNK
 PIECES = (2, 2, 2, 2)
 LEAD_CAST, LEAD_QUANT, LEAD_FILTER, LAG = 4, 3, 2, 1
 GATHER = 512
-W2_AFTER = 1
+W2_AFTER = 3
+W2_STEP = 2
 HALF = H // 2
 OUT_GROUPS = ((0, 1), (2, 3), (4, 5), (6,), (7,))
 E_GROUPS = (((0,), "scalar"), ((1,), "scalar"), ((2,), "vector"), ((3,), "scalar"), ((4,), "scalar"), ((5,), "scalar"), ((6,), "vector"), ((7,), "scalar"))
@@ -69,12 +70,12 @@ def tile_picked_schnet_gelu_p_kernel(tc, x_words, x_scales, eT, w1, w3, w2, offs
         def mx_tiles(name, width):
             return sb(name + "_codes", [P, width], U32), sb(name + "_scales", [P, width], U8)
 
-        def deal(engine, dealt, raw, m0, u):
-            ms = raw.shape[2] // PACK
+        def deal(engine, dealt, raw, a0, u):
+            runs = raw.shape[2] // 16
             copy_on(
                 engine,
-                dealt[:].rearrange("p (t m j) -> p m j t", t=2, j=PACK)[:, m0 : m0 + ms, :, :],
-                raw.rearrange("p j (m t) -> p m j t", t=PACK)[:, :, :, 2 * u : 2 * u + 2],
+                dealt[:].rearrange("p (t a q j) -> p a t j q", t=2, q=4, j=PACK)[:, a0 : a0 + runs],
+                raw.rearrange("p j (a t q) -> p a t j q", t=PACK, q=4)[:, :, 2 * u : 2 * u + 2],
             )
 
         def quantize_dealt(w_mx, dealt):
@@ -158,8 +159,8 @@ def tile_picked_schnet_gelu_p_kernel(tc, x_words, x_scales, eT, w1, w3, w2, offs
                 mx(acc[:, t, :], w3_mx, slice(t * P, (t + 1) * P), tiles, slice(at, at + CHUNK))
             gate[c] = sb("gate%d" % c, [P, CHUNK * PACK], F32)
             nc.scalar.activation(
-                out=gate[c][:].rearrange("p (n t) -> p n t", t=PACK),
-                in_=acc[:].rearrange("p t n -> p n t"),
+                out=gate[c][:].rearrange("p (a t i) -> p a t i", t=PACK, i=2),
+                in_=acc[:].rearrange("p t (a i) -> p a t i", i=2),
                 func=GELU,
                 bias=zero_bias[:],
             )
@@ -185,16 +186,18 @@ def tile_picked_schnet_gelu_p_kernel(tc, x_words, x_scales, eT, w1, w3, w2, offs
                 z_tiles[g] = sb("z%d" % c, [P, len(g) * CHUNK * PACK], BF16)
             at = (c - g[0]) * CHUNK * PACK
             nc.vector.tensor_tensor(
-                out=z_tiles[g][:, at : at + CHUNK * PACK].rearrange("p (n t) -> p n t", t=PACK),
-                in0=c_acc[c][:].rearrange("p t n -> p n t"),
-                in1=gate[c][:].rearrange("p (n t) -> p n t", t=PACK),
+                out=z_tiles[g][:, at : at + CHUNK * PACK].rearrange("p (a i t) -> p a t i", t=PACK, i=2),
+                in0=c_acc[c][:].rearrange("p t (a i) -> p a t i", i=2),
+                in1=gate[c][:].rearrange("p (a t i) -> p a t i", t=PACK, i=2),
                 op=MULT,
             )
 
+        def quantize_z(g):
+            z_mx[g] = mx_tiles("z%d" % g[0], len(g) * CHUNK)
+            quantize(z_mx[g][0][:], z_mx[g][1][:], z_tiles[g][:])
+
         def project(g):
             width = len(g) * CHUNK
-            z_mx[g] = mx_tiles("z%d" % g[0], width)
-            quantize(z_mx[g][0][:], z_mx[g][1][:], z_tiles[g][:])
             acc = psum.tile([P, 2 * CHUNK], F32, name="o_acc", tag="o_acc", bufs=2)
             mx(acc[:, 0:width], w2_mx, slice(0, N), z_mx[g], slice(0, width))
             res = sb("res%d" % g[0], [P, width], F32)
@@ -219,7 +222,9 @@ def tile_picked_schnet_gelu_p_kernel(tc, x_words, x_scales, eT, w1, w3, w2, offs
             e_raw.append(load_into(late[:, at : at + PACK * PIECES[i] * CHUNK], eT, piece_cols(i)))
             at = at + PACK * PIECES[i] * CHUNK
             if i == W2_AFTER:
-                w2_raw = load_into(late[:, at : at + PACK * N], w2, slice(0, N))
+                w2_raw = late[:, at : at + PACK * N].rearrange("p (t n) -> p t n", t=PACK)
+                for t in range(PACK):
+                    nc.sync.dma_start(out=w2_raw[:, t, :], in_=w2.rearrange("(a t q) n -> t a q n", t=PACK, q=4)[t])
                 at = at + PACK * N
         picked_words = []
         for h in range(S // GATHER):
@@ -231,12 +236,13 @@ def tile_picked_schnet_gelu_p_kernel(tc, x_words, x_scales, eT, w1, w3, w2, offs
         w1_dealt = [sb("w1_dealt%d" % u, [P, 2 * P * PACK], BF16) for u in range(2)]
         for h in range(2):
             for u in range(2):
-                deal("vector" if (h, u) == (1, 0) else "scalar", w1_dealt[u], w1_raw[h], h * HALF // PACK, u)
+                deal("vector" if (h, u) == (1, 0) else "scalar", w1_dealt[u], w1_raw[h], h * HALF // 16, u)
         quantize_dealt(w1_mx, w1_dealt)
 
         w2_mx = mx_tiles("w2", N)
 
         first = PIECES[0]
+        waiting = []
         for step in range(-max(LEAD_CAST, LEAD_QUANT, LEAD_FILTER), CHUNKS + LAG):
             if 0 <= step + 1 < CHUNKS:
                 atoms_of(step + 1)
@@ -248,10 +254,15 @@ def tile_picked_schnet_gelu_p_kernel(tc, x_words, x_scales, eT, w1, w3, w2, offs
                 filter_of(step + LEAD_FILTER)
             if 0 <= step < CHUNKS:
                 message(step)
-            if step == 0:
+            if step == W2_STEP:
                 w2_woven = weave("w2_woven", "scalar", w2_raw)
-            if step == 1:
+            if step == W2_STEP + 1:
                 quantize(w2_mx[0][:], w2_mx[1][:], w2_woven[:])
             done = step - LAG
             if 0 <= done and group_of[done][-1] == done:
-                project(group_of[done])
+                quantize_z(group_of[done])
+                waiting.append(group_of[done])
+            if step > W2_STEP:
+                for g in waiting:
+                    project(g)
+                waiting.clear()

@@ -17,16 +17,18 @@ MULT = mybir.AluOpType.mult
 
 P = 128
 PACK = 4
+QUADRANT = 32
+SPREAD = 8
+LIST_ROWS = 16
 CHUNK = 128
 CHUNKS = S // CHUNK
-PIECES = (2, 2, 2, 2)
-LEAD_CAST, LEAD_QUANT, LEAD_FILTER, LAG = 4, 3, 2, 1
+PIECE = 2 * CHUNK
+PIECES = S // PIECE
 GATHER = 512
-W2_AFTER = 3
-W2_STEP = 2
 HALF = H // 2
-OUT_GROUPS = ((0, 1), (2, 3), (4, 5), (6,), (7,))
-E_GROUPS = (((0,), "scalar"), ((1,), "scalar"), ((2,), "vector"), ((3,), "scalar"), ((4,), "scalar"), ((5,), "scalar"), ((6,), "vector"), ((7,), "scalar"))
+LEAD_ROUND, LEAD_QUANTISE, LEAD_FILTER = 4, 3, 2
+OUT_GROUPS = ((0, 1, 2, 3), (4, 5), (6,), (7,))
+FILTER_BANKS, ATOM_BANKS = 4, 3
 
 
 def tile_picked_schnet_gelu_p_kernel(tc, x_words, x_scales, eT, w1, w3, w2, offs, out):
@@ -38,231 +40,205 @@ def tile_picked_schnet_gelu_p_kernel(tc, x_words, x_scales, eT, w1, w3, w2, offs
         def sb(name, shape, dtype, slot=None):
             return keep.tile(shape, dtype, name=name, tag=slot or name, align_bytes=64)
 
-        def copy_on(engine, dst, src):
-            if engine == "vector":
-                nc.vector.tensor_copy(out=dst, in_=src)
-            else:
-                nc.scalar.copy(out=dst, in_=src)
+        def mx_tiles(name, width):
+            return sb(name + "_words", [P, width], U32), sb(name + "_scales", [P, width], U8)
 
-        def quantize(codes, scales, values):
-            nc.vector.quantize_mx(out=codes.bitcast(FP8X4), scales=scales, in_=values)
+        def quantise(words, scales, values):
+            nc.vector.quantize_mx(out=words.bitcast(FP8X4), scales=scales, in_=values)
 
-        def mx(acc, lhs, lhs_cols, rhs, rhs_cols):
+        def product(acc, weight, weight_cols, words, scales):
             nc.tensor.matmul_mx(
                 out=acc,
-                lhsT=lhs[0][:, lhs_cols].bitcast(FP8X4),
-                lhsT_scale=lhs[1][:, lhs_cols],
-                rhs=rhs[0][:, rhs_cols].bitcast(FP8X4),
-                rhs_scale=rhs[1][:, rhs_cols],
+                lhsT=weight[0][:, weight_cols].bitcast(FP8X4),
+                lhsT_scale=weight[1][:, weight_cols],
+                rhs=words.bitcast(FP8X4),
+                rhs_scale=scales,
                 start=True,
                 stop=True,
             )
 
-        def load_into(flat, src, cols):
+        def load_rows(flat, src, cols):
             raw = flat.rearrange("p (j c) -> p j c", j=PACK)
             nc.sync.dma_start(out=raw, in_=src.rearrange("(p j) c -> p j c", j=PACK)[:, :, cols])
             return raw
 
-        def load_rows(name, src, cols, slot):
-            flat = sb(name, [P, PACK * (cols.stop - cols.start)], F32, slot)
-            return load_into(flat[:], src, cols)
-
-        def mx_tiles(name, width):
-            return sb(name + "_codes", [P, width], U32), sb(name + "_scales", [P, width], U8)
-
-        def deal(engine, dealt, raw, a0, u):
-            runs = raw.shape[2] // 16
-            copy_on(
-                engine,
-                dealt[:].rearrange("p (t a q j) -> p a t j q", t=2, q=4, j=PACK)[:, a0 : a0 + runs],
-                raw.rearrange("p j (a t q) -> p a t j q", t=PACK, q=4)[:, :, 2 * u : 2 * u + 2],
-            )
-
-        def quantize_dealt(w_mx, dealt):
-            for t in range(PACK):
-                cols = slice(t * P, (t + 1) * P)
-                at = (t % 2) * P * PACK
-                quantize(w_mx[0][:, cols], w_mx[1][:, cols], dealt[t // 2][:, at : at + P * PACK])
-
-        def weave(name, engine, raw_cols, slot=None):
-            width = raw_cols.shape[2]
-            woven = sb(name, [P, width * PACK], BF16, slot)
-            copy_on(
-                engine,
-                woven[:].rearrange("p (c i j) -> p c j i", i=4, j=PACK),
-                raw_cols.rearrange("p j (c i) -> p c j i", i=4),
+        def weave(copy, name, raw):
+            woven = sb(name, [P, raw.shape[2] * PACK], BF16)
+            copy(
+                out=woven[:].rearrange("p (c i j) -> p c j i", i=4, j=PACK),
+                in_=raw.rearrange("p j (c i) -> p c j i", i=4),
             )
             return woven
 
-        def half_cols(h):
-            return slice(h * HALF, (h + 1) * HALF)
+        def deal(copy, dealt, raw, m0, u):
+            copy(
+                out=dealt[:].rearrange("p (t m j) -> p m j t", t=2, j=PACK)[:, m0 : m0 + raw.shape[2] // PACK, :, :],
+                in_=raw.rearrange("p j (m t) -> p m j t", t=PACK)[:, :, :, 2 * u : 2 * u + 2],
+            )
 
-        def piece_cols(i):
-            return slice(sum(PIECES[:i]) * CHUNK, sum(PIECES[: i + 1]) * CHUNK)
+        def in_pairs(bank):
+            return bank.rearrange("p t (a i) -> p a t i", i=2)
 
-        table_scales = sb("table_scales", [P, T], U8, "scale_table")
+        def edge_cols(piece):
+            return slice(piece * PIECE, (piece + 1) * PIECE)
+
+        table_scales = sb("table_scales", [P, T], U8, "scale_slot")
         nc.vector.memset(table_scales[:].bitcast(I32), 0)
-        zero_in = sb("zero_in", [P, 1], F32, "table")
-        nc.vector.memset(zero_in[:], 0.0)
+        zero_seed = sb("zero_seed", [P, 1], F32, "word_slot")
+        nc.vector.memset(zero_seed[:], 0.0)
+        zero_in = sb("zero_in", [P, 1], F32)
+        nc.vector.tensor_copy(out=zero_in[:], in_=zero_seed[:])
         zero_bias = sb("zero_bias", [P, 1], F32)
         nc.scalar.activation(out=zero_bias[:], in_=zero_in[:], func=GELU)
 
-        w3_raw = load_rows("w3_raw", w3, slice(0, H), "w_stage")
-        offsets = keep.tile([P, S // 16], U16, name="offsets")
+        w3_stage = sb("w3_stage", [P, PACK * H], F32, "weight_slot")
+        w3_raw = load_rows(w3_stage[:], w3, slice(0, H))
+        offsets = keep.tile([P, S // LIST_ROWS], U16, name="offsets")
         nc.sync.dma_start(offsets[:], offs)
-        e_raw = [load_rows("e_raw0", eT, piece_cols(0), "e_stage")]
-        nc.sync.dma_start(out=table_scales[0:P:8, :].bitcast(I32), in_=x_scales[0].bitcast(I32))
-        table_words = sb("table_words", [P, T], U32, "table")
+        first_stage = sb("first_stage", [P, PACK * PIECE], F32)
+        e_raw = [load_rows(first_stage[:], eT, edge_cols(0))]
+        nc.sync.dma_start(out=table_scales[0:P:SPREAD, :].bitcast(I32), in_=x_scales[0].bitcast(I32))
+        table_words = sb("table_words", [P, T], U32, "word_slot")
         nc.sync.dma_start(out=table_words[:].bitcast(I32), in_=x_words[0].rearrange("p c r -> p (c r)").bitcast(I32))
         placed_scales = sb("placed_scales", [P, S], U8)
         nc.vector.memset(placed_scales[:].bitcast(I32), 0)
 
         w3_mx = mx_tiles("w3", H)
         w3_dealt = [sb("w3_dealt%d" % u, [P, 2 * P * PACK], BF16) for u in range(2)]
-        deal("vector", w3_dealt[0], w3_raw, 0, 0)
-        deal("scalar", w3_dealt[1], w3_raw, 0, 1)
+        deal(nc.vector.tensor_copy, w3_dealt[0], w3_raw, 0, 0)
+        deal(nc.scalar.copy, w3_dealt[1], w3_raw, 0, 1)
         for u in range(2):
             cols = slice(2 * u * P, 2 * (u + 1) * P)
-            quantize(w3_mx[0][:, cols], w3_mx[1][:, cols], w3_dealt[u][:])
-        w1_raw = [load_rows("w1_raw0", w1, half_cols(0), "w_stage"), load_rows("w1_raw1", w1, half_cols(1), "w3_dealt1")]
-
-        e_mx = {}
-        gate = {}
-        c_acc = {}
-        z_tiles = {}
-        z_mx = {}
-        group_of = {c: g for g in OUT_GROUPS for c in g}
+            quantise(w3_mx[0][:, cols], w3_mx[1][:, cols], w3_dealt[u][:])
+        w1_stage = sb("w1_stage", [P, PACK * H], F32, "weight_slot")
+        w1_raw = [
+            load_rows(w1_stage[:, h * PACK * HALF : (h + 1) * PACK * HALF], w1, slice(h * HALF, (h + 1) * HALF))
+            for h in range(2)
+        ]
 
         e_woven = {}
+        e_mx = {}
+        gates = {}
+        atom_acc = {}
+        z_values = {}
+        group_of = {c: group for group in OUT_GROUPS for c in group}
 
-        e_group_at = {g[0]: (g, engine) for g, engine in E_GROUPS}
+        def round_edges(c):
+            piece, second = divmod(c, 2)
+            if piece % 2 == 1:
+                copy = nc.scalar.copy if second else nc.vector.tensor_copy
+                e_woven[c] = weave(copy, "e_woven%d" % c, e_raw[piece][:, :, second * CHUNK : (second + 1) * CHUNK])
+            elif not second:
+                e_woven[c] = weave(nc.scalar.copy, "e_woven%d" % c, e_raw[piece])
 
-        def cast_e(c):
-            if c in e_group_at:
-                g, engine = e_group_at[c]
-                piece = max(i for i in range(len(PIECES)) if sum(PIECES[:i]) <= c)
-                at = (c - sum(PIECES[:piece])) * CHUNK
-                e_woven[c] = weave("e_woven%d" % c, engine, e_raw[piece][:, :, at : at + len(g) * CHUNK])
+        def quantise_edges(c):
+            if c in e_woven:
+                width = e_woven[c].shape[1] // PACK
+                words, scales = mx_tiles("e%d" % c, width)
+                quantise(words[:], scales[:], e_woven[c][:])
+                for at in range(0, width, CHUNK):
+                    e_mx[c + at // CHUNK] = (words[:, at : at + CHUNK], scales[:, at : at + CHUNK])
 
-        def quantize_e(c):
-            if c in e_group_at:
-                g = e_group_at[c][0]
-                tiles = mx_tiles("e%d" % c, len(g) * CHUNK)
-                quantize(tiles[0][:], tiles[1][:], e_woven[c][:])
-                for member in g:
-                    e_mx[member] = (tiles, (member - c) * CHUNK)
-
-        def filter_of(c):
-            acc = psum.tile([P, PACK, CHUNK], F32, name="f_acc", tag="f_acc", bufs=3)
-            tiles, at = e_mx[c]
+        def filter_edges(c):
+            acc = psum.tile([P, PACK, CHUNK], F32, name="filter_acc", tag="filter", bufs=FILTER_BANKS)
             for t in range(PACK):
-                mx(acc[:, t, :], w3_mx, slice(t * P, (t + 1) * P), tiles, slice(at, at + CHUNK))
-            gate[c] = sb("gate%d" % c, [P, CHUNK * PACK], F32)
+                product(acc[:, t, :], w3_mx, slice(t * P, (t + 1) * P), *e_mx[c])
+            gates[c] = sb("gate%d" % c, [P, CHUNK * PACK], F32)
             nc.scalar.activation(
-                out=gate[c][:].rearrange("p (a t i) -> p a t i", t=PACK, i=2),
-                in_=acc[:].rearrange("p t (a i) -> p a t i", i=2),
+                out=gates[c][:].rearrange("p (a t i) -> p a t i", t=PACK, i=2),
+                in_=in_pairs(acc[:]),
                 func=GELU,
                 bias=zero_bias[:],
             )
 
-        def atoms_of(c):
-            acc = psum.tile([P, PACK, CHUNK], F32, name="c_acc", tag="c_acc", bufs=3)
-            half, at = divmod(c * CHUNK, GATHER)
+        def multiply_atoms(c):
+            acc = psum.tile([P, PACK, CHUNK], F32, name="atom_acc", tag="atom", bufs=ATOM_BANKS)
+            part, at = divmod(c * CHUNK, GATHER)
             for t in range(PACK):
-                nc.tensor.matmul_mx(
-                    out=acc[:, t, :],
-                    lhsT=w1_mx[0][:, t * P : (t + 1) * P].bitcast(FP8X4),
-                    lhsT_scale=w1_mx[1][:, t * P : (t + 1) * P],
-                    rhs=picked_words[half][:, at : at + CHUNK].bitcast(FP8X4),
-                    rhs_scale=placed_scales[:, c * CHUNK : (c + 1) * CHUNK],
-                    start=True,
-                    stop=True,
+                product(
+                    acc[:, t, :],
+                    w1_mx,
+                    slice(t * P, (t + 1) * P),
+                    picked_words[part][:, at : at + CHUNK],
+                    placed_scales[:, c * CHUNK : (c + 1) * CHUNK],
                 )
-            c_acc[c] = acc
+            atom_acc[c] = acc
 
         def message(c):
-            g = group_of[c]
-            if g not in z_tiles:
-                z_tiles[g] = sb("z%d" % c, [P, len(g) * CHUNK * PACK], BF16)
-            at = (c - g[0]) * CHUNK * PACK
+            group = group_of[c]
+            if c == group[0]:
+                z_values[group] = sb("z%d" % c, [P, len(group) * CHUNK * PACK], BF16)
+            at = (c - group[0]) * CHUNK * PACK
             nc.vector.tensor_tensor(
-                out=z_tiles[g][:, at : at + CHUNK * PACK].rearrange("p (a i t) -> p a t i", t=PACK, i=2),
-                in0=c_acc[c][:].rearrange("p t (a i) -> p a t i", i=2),
-                in1=gate[c][:].rearrange("p (a t i) -> p a t i", t=PACK, i=2),
+                out=z_values[group][:, at : at + CHUNK * PACK].rearrange("p (a i t) -> p a t i", t=PACK, i=2),
+                in0=in_pairs(atom_acc[c][:]),
+                in1=gates[c][:].rearrange("p (a t i) -> p a t i", t=PACK, i=2),
                 op=MULT,
             )
 
-        def quantize_z(g):
-            z_mx[g] = mx_tiles("z%d" % g[0], len(g) * CHUNK)
-            quantize(z_mx[g][0][:], z_mx[g][1][:], z_tiles[g][:])
+        def project(group):
+            width = len(group) * CHUNK
+            words, scales = mx_tiles("z%d" % group[0], width)
+            quantise(words[:], scales[:], z_values[group][:])
+            if group == OUT_GROUPS[0]:
+                acc = psum.tile([P, width], F32, name="out_acc", tag="out", bufs=1)
+            else:
+                acc = psum.tile([P, width], F32, name="out_acc", tag="filter", bufs=FILTER_BANKS)
+            product(acc[:], w2_mx, slice(0, N), words[:], scales[:])
+            result = sb("result%d" % group[0], [P, width], F32)
+            nc.scalar.copy(out=result[:], in_=acc[:])
+            nc.sync.dma_start(out=out[:, group[0] * CHUNK : group[0] * CHUNK + width], in_=result[:])
 
-        def project(g):
-            width = len(g) * CHUNK
-            acc = psum.tile([P, 2 * CHUNK], F32, name="o_acc", tag="o_acc", bufs=2)
-            mx(acc[:, 0:width], w2_mx, slice(0, N), z_mx[g], slice(0, width))
-            res = sb("res%d" % g[0], [P, width], F32)
-            nc.scalar.copy(out=res[:], in_=acc[:, 0:width])
-            queue = nc.scalar if g == OUT_GROUPS[-1] else nc.sync
-            queue.dma_start(out=out[:, g[0] * CHUNK : g[0] * CHUNK + width], in_=res[:])
-
-        for c in range(PIECES[0]):
-            cast_e(c)
-        for c in range(PIECES[0]):
-            quantize_e(c)
-        for c in range(PIECES[0]):
-            filter_of(c)
+        first = PIECE // CHUNK
+        round_edges(0)
+        quantise_edges(0)
+        for c in range(first):
+            filter_edges(c)
 
         picked_scales = sb("picked_scales", [P, S], U8)
         nc.vector.tensor_copy(picked_scales[:], table_scales[:].indirect(offsets[:]))
-        for r in range(4):
-            nc.sync.dma_start(out=placed_scales[r:P:32, :].bitcast(I32), in_=picked_scales[8 * r : P : 32, :].bitcast(I32))
-        late = sb("late", [P, PACK * (S - PIECES[0] * CHUNK + N)], F32, "scale_table")
-        at = 0
-        for i in range(1, len(PIECES)):
-            e_raw.append(load_into(late[:, at : at + PACK * PIECES[i] * CHUNK], eT, piece_cols(i)))
-            at = at + PACK * PIECES[i] * CHUNK
-            if i == W2_AFTER:
-                w2_raw = late[:, at : at + PACK * N].rearrange("p (t n) -> p t n", t=PACK)
-                for t in range(PACK):
-                    nc.sync.dma_start(out=w2_raw[:, t, :], in_=w2.rearrange("(a t q) n -> t a q n", t=PACK, q=4)[t])
-                at = at + PACK * N
+        for r in range(QUADRANT // SPREAD):
+            nc.sync.dma_start(
+                out=placed_scales[r:P:QUADRANT, :].bitcast(I32),
+                in_=picked_scales[SPREAD * r : P : QUADRANT, :].bitcast(I32),
+            )
+        late_stage = sb("late_stage", [P, PACK * (S - PIECE + N)], F32, "scale_slot")
+        for piece in range(1, PIECES):
+            at = (piece - 1) * PACK * PIECE
+            e_raw.append(load_rows(late_stage[:, at : at + PACK * PIECE], eT, edge_cols(piece)))
+        w2_raw = load_rows(late_stage[:, PACK * (S - PIECE) :], w2, slice(0, N))
         picked_words = []
-        for h in range(S // GATHER):
-            words = sb("picked_words%d" % h, [P, GATHER], U32)
-            nc.vector.tensor_copy(words[:], table_words[:].indirect(offsets[:, h * GATHER // 16 : (h + 1) * GATHER // 16]))
+        for part in range(S // GATHER):
+            words = sb("picked_words%d" % part, [P, GATHER], U32)
+            entries = offsets[:, part * GATHER // LIST_ROWS : (part + 1) * GATHER // LIST_ROWS]
+            nc.vector.tensor_copy(words[:], table_words[:].indirect(entries))
             picked_words.append(words)
 
         w1_mx = mx_tiles("w1", H)
         w1_dealt = [sb("w1_dealt%d" % u, [P, 2 * P * PACK], BF16) for u in range(2)]
-        for h in range(2):
-            for u in range(2):
-                deal("vector" if (h, u) == (1, 0) else "scalar", w1_dealt[u], w1_raw[h], h * HALF // 16, u)
-        quantize_dealt(w1_mx, w1_dealt)
+        for u in range(2):
+            deal(nc.scalar.copy, w1_dealt[u], w1_raw[0], 0, u)
+        deal(nc.vector.tensor_copy, w1_dealt[0], w1_raw[1], HALF // PACK, 0)
+        deal(nc.scalar.copy, w1_dealt[1], w1_raw[1], HALF // PACK, 1)
+        for t in range(PACK):
+            cols = slice(t * P, (t + 1) * P)
+            at = (t % 2) * P * PACK
+            quantise(w1_mx[0][:, cols], w1_mx[1][:, cols], w1_dealt[t // 2][:, at : at + P * PACK])
 
         w2_mx = mx_tiles("w2", N)
-
-        first = PIECES[0]
-        waiting = []
-        for step in range(-max(LEAD_CAST, LEAD_QUANT, LEAD_FILTER), CHUNKS + LAG):
+        for step in range(first - LEAD_ROUND, CHUNKS + 1):
             if 0 <= step + 1 < CHUNKS:
-                atoms_of(step + 1)
-            if first <= step + LEAD_CAST < CHUNKS:
-                cast_e(step + LEAD_CAST)
-            if first <= step + LEAD_QUANT < CHUNKS:
-                quantize_e(step + LEAD_QUANT)
+                multiply_atoms(step + 1)
+            if step + LEAD_ROUND < CHUNKS:
+                round_edges(step + LEAD_ROUND)
+            if first <= step + LEAD_QUANTISE < CHUNKS:
+                quantise_edges(step + LEAD_QUANTISE)
             if first <= step + LEAD_FILTER < CHUNKS:
-                filter_of(step + LEAD_FILTER)
+                filter_edges(step + LEAD_FILTER)
             if 0 <= step < CHUNKS:
                 message(step)
-            if step == W2_STEP:
-                w2_woven = weave("w2_woven", "scalar", w2_raw)
-            if step == W2_STEP + 1:
-                quantize(w2_mx[0][:], w2_mx[1][:], w2_woven[:])
-            done = step - LAG
-            if 0 <= done and group_of[done][-1] == done:
-                quantize_z(group_of[done])
-                waiting.append(group_of[done])
-            if step > W2_STEP:
-                for g in waiting:
-                    project(g)
-                waiting.clear()
+            if step == OUT_GROUPS[0][-1]:
+                w2_woven = weave(nc.scalar.copy, "w2_woven", w2_raw)
+                quantise(w2_mx[0][:], w2_mx[1][:], w2_woven[:])
+            if step >= 1 and group_of[step - 1][-1] == step - 1:
+                project(group_of[step - 1])

@@ -214,6 +214,10 @@ def tile_picked_schnet_gelu_p_kernel(tc, x_words, x_scales, eT, w1, w3, w2, offs
             nc.vector.tensor_copy(words[:], table_words[:].indirect(entries))
             picked_words.append(words)
 
+        warm = psum.tile([P, GATHER], F32, name="out_acc", tag="out", bufs=1)
+        for t in range(PACK):
+            product(warm[:], w3_mx, slice(t * P, (t + 1) * P), picked_words[0][:], picked_scales[:, 0:GATHER])
+
         w1_mx = mx_tiles("w1", H)
         w1_dealt = [sb("w1_dealt%d" % u, [P, 2 * P * PACK], BF16) for u in range(2)]
         for u in range(2):

from contextlib import ExitStack

import concourse.mybir as mybir

K, T, S, J, H, N = 512, 4096, 1024, 512, 512, 128
FLOPS = 2 * S * (K * H + J * H + H * N)

F32 = mybir.dt.float32
BF16 = mybir.dt.bfloat16
I32 = mybir.dt.int32
U32 = mybir.dt.uint32
U16 = mybir.dt.uint16
U8 = mybir.dt.uint8
FP8X4 = mybir.dt.float8_e4m3fn_x4
GELU = mybir.ActivationFunctionType.Gelu_apprx_tanh
MULT = mybir.AluOpType.mult

P = 128
PACK = 4
QUADRANT = 32
SPREAD = 8
LIST_ROWS = 16
CHUNK = 128
CHUNKS = S // CHUNK
PIECE = 2 * CHUNK
PIECES = S // PIECE
GATHER = 512
HALF = H // 2
LEAD_ROUND, LEAD_QUANTISE, LEAD_FILTER = 4, 3, 2
OUT_GROUPS = ((0, 1, 2, 3), (4, 5), (6,), (7,))
FILTER_BANKS, ATOM_BANKS = 4, 3


def tile_picked_schnet_gelu_p_kernel(tc, x_words, x_scales, eT, w1, w3, w2, offs, out):
    nc = tc.nc
    with ExitStack() as ctx:
        keep = ctx.enter_context(tc.tile_pool(name="keep", bufs=1))
        psum = ctx.enter_context(tc.psum_pool(name="psum", bufs=1))

        def sb(name, shape, dtype, slot=None):
            return keep.tile(shape, dtype, name=name, tag=slot or name, align_bytes=64)

        def mx_tiles(name, width):
            return sb(name + "_words", [P, width], U32), sb(name + "_scales", [P, width], U8)

        def quantise(words, scales, values):
            nc.vector.quantize_mx(out=words.bitcast(FP8X4), scales=scales, in_=values)

        def product(acc, weight, weight_cols, words, scales):
            nc.tensor.matmul_mx(
                out=acc,
                lhsT=weight[0][:, weight_cols].bitcast(FP8X4),
                lhsT_scale=weight[1][:, weight_cols],
                rhs=words.bitcast(FP8X4),
                rhs_scale=scales,
                start=True,
                stop=True,
            )

        def load_rows(flat, src, cols):
            raw = flat.rearrange("p (j c) -> p j c", j=PACK)
            nc.sync.dma_start(out=raw, in_=src.rearrange("(p j) c -> p j c", j=PACK)[:, :, cols])
            return raw

        def weave(copy, name, raw):
            woven = sb(name, [P, raw.shape[2] * PACK], BF16)
            copy(
                out=woven[:].rearrange("p (c i j) -> p c j i", i=4, j=PACK),
                in_=raw.rearrange("p j (c i) -> p c j i", i=4),
            )
            return woven

        def deal(copy, dealt, raw, m0, u):
            copy(
                out=dealt[:].rearrange("p (t m j) -> p m j t", t=2, j=PACK)[:, m0 : m0 + raw.shape[2] // PACK, :, :],
                in_=raw.rearrange("p j (m t) -> p m j t", t=PACK)[:, :, :, 2 * u : 2 * u + 2],
            )

        def in_pairs(bank):
            return bank.rearrange("p t (a i) -> p a t i", i=2)

        def edge_cols(piece):
            return slice(piece * PIECE, (piece + 1) * PIECE)

        table_scales = sb("table_scales", [P, T], U8, "scale_slot")
        nc.vector.memset(table_scales[:].bitcast(I32), 0)
        zero_seed = sb("zero_seed", [P, 1], F32, "word_slot")
        nc.vector.memset(zero_seed[:], 0.0)
        zero_in = sb("zero_in", [P, 1], F32)
        nc.vector.tensor_copy(out=zero_in[:], in_=zero_seed[:])
        zero_bias = sb("zero_bias", [P, 1], F32)
        nc.scalar.activation(out=zero_bias[:], in_=zero_in[:], func=GELU)

        w3_stage = sb("w3_stage", [P, PACK * H], F32, "weight_slot")
        w3_raw = load_rows(w3_stage[:], w3, slice(0, H))
        offsets = keep.tile([P, S // LIST_ROWS], U16, name="offsets")
        nc.sync.dma_start(offsets[:], offs)
        first_stage = sb("first_stage", [P, PACK * PIECE], F32)
        e_raw = [load_rows(first_stage[:], eT, edge_cols(0))]
        nc.sync.dma_start(out=table_scales[0:P:SPREAD, :].bitcast(I32), in_=x_scales[0].bitcast(I32))
        table_words = sb("table_words", [P, T], U32, "word_slot")
        nc.sync.dma_start(out=table_words[:].bitcast(I32), in_=x_words[0].rearrange("p c r -> p (c r)").bitcast(I32))
        placed_scales = sb("placed_scales", [P, S], U8)
        nc.vector.memset(placed_scales[:].bitcast(I32), 0)

        w3_mx = mx_tiles("w3", H)
        w3_dealt = [sb("w3_dealt%d" % u, [P, 2 * P * PACK], BF16) for u in range(2)]
        deal(nc.vector.tensor_copy, w3_dealt[0], w3_raw, 0, 0)
        deal(nc.scalar.copy, w3_dealt[1], w3_raw, 0, 1)
        for u in range(2):
            cols = slice(2 * u * P, 2 * (u + 1) * P)
            quantise(w3_mx[0][:, cols], w3_mx[1][:, cols], w3_dealt[u][:])
        w1_stage = sb("w1_stage", [P, PACK * H], F32, "weight_slot")
        w1_raw = [
            load_rows(w1_stage[:, h * PACK * HALF : (h + 1) * PACK * HALF], w1, slice(h * HALF, (h + 1) * HALF))
            for h in range(2)
        ]

        e_woven = {}
        e_mx = {}
        gates = {}
        atom_acc = {}
        z_values = {}
        group_of = {c: group for group in OUT_GROUPS for c in group}

        def round_edges(c):
            piece, second = divmod(c, 2)
            if piece % 2 == 1:
                copy = nc.scalar.copy if second else nc.vector.tensor_copy
                e_woven[c] = weave(copy, "e_woven%d" % c, e_raw[piece][:, :, second * CHUNK : (second + 1) * CHUNK])
            elif not second:
                e_woven[c] = weave(nc.scalar.copy, "e_woven%d" % c, e_raw[piece])

        def quantise_edges(c):
            if c in e_woven:
                width = e_woven[c].shape[1] // PACK
                words, scales = mx_tiles("e%d" % c, width)
                quantise(words[:], scales[:], e_woven[c][:])
                for at in range(0, width, CHUNK):
                    e_mx[c + at // CHUNK] = (words[:, at : at + CHUNK], scales[:, at : at + CHUNK])

        def filter_edges(c):
            acc = psum.tile([P, PACK, CHUNK], F32, name="filter_acc", tag="filter", bufs=FILTER_BANKS)
            for t in range(PACK):
                product(acc[:, t, :], w3_mx, slice(t * P, (t + 1) * P), *e_mx[c])
            gates[c] = sb("gate%d" % c, [P, CHUNK * PACK], F32)
            nc.scalar.activation(
                out=gates[c][:].rearrange("p (a t i) -> p a t i", t=PACK, i=2),
                in_=in_pairs(acc[:]),
                func=GELU,
                bias=zero_bias[:],
            )

        def multiply_atoms(c):
            acc = psum.tile([P, PACK, CHUNK], F32, name="atom_acc", tag="atom", bufs=ATOM_BANKS)
            part, at = divmod(c * CHUNK, GATHER)
            for t in range(PACK):
                product(
                    acc[:, t, :],
                    w1_mx,
                    slice(t * P, (t + 1) * P),
                    picked_words[part][:, at : at + CHUNK],
                    placed_scales[:, c * CHUNK : (c + 1) * CHUNK],
                )
            atom_acc[c] = acc

        def message(c):
            group = group_of[c]
            if c == group[0]:
                z_values[group] = sb("z%d" % c, [P, len(group) * CHUNK * PACK], BF16)
            at = (c - group[0]) * CHUNK * PACK
            nc.vector.tensor_tensor(
                out=z_values[group][:, at : at + CHUNK * PACK].rearrange("p (a i t) -> p a t i", t=PACK, i=2),
                in0=in_pairs(atom_acc[c][:]),
                in1=gates[c][:].rearrange("p (a t i) -> p a t i", t=PACK, i=2),
                op=MULT,
            )

        def project(group):
            width = len(group) * CHUNK
            words, scales = mx_tiles("z%d" % group[0], width)
            quantise(words[:], scales[:], z_values[group][:])
            if group == OUT_GROUPS[0]:
                acc = psum.tile([P, width], F32, name="out_acc", tag="out", bufs=1)
            else:
                acc = psum.tile([P, width], F32, name="out_acc", tag="filter", bufs=FILTER_BANKS)
            product(acc[:], w2_mx, slice(0, N), words[:], scales[:])
            result = sb("result%d" % group[0], [P, width], F32)
            nc.scalar.copy(out=result[:], in_=acc[:])
            nc.sync.dma_start(out=out[:, group[0] * CHUNK : group[0] * CHUNK + width], in_=result[:])

        first = PIECE // CHUNK
        round_edges(0)
        quantise_edges(0)
        for c in range(first):
            filter_edges(c)

        picked_scales = sb("picked_scales", [P, S], U8)
        nc.vector.tensor_copy(picked_scales[:], table_scales[:].indirect(offsets[:]))
        for r in range(QUADRANT // SPREAD):
            nc.sync.dma_start(
                out=placed_scales[r:P:QUADRANT, :].bitcast(I32),
                in_=picked_scales[SPREAD * r : P : QUADRANT, :].bitcast(I32),
            )
        late_stage = sb("late_stage", [P, PACK * (S - PIECE + N)], F32, "scale_slot")
        for piece in range(1, PIECES):
            at = (piece - 1) * PACK * PIECE
            e_raw.append(load_rows(late_stage[:, at : at + PACK * PIECE], eT, edge_cols(piece)))
        w2_raw = load_rows(late_stage[:, PACK * (S - PIECE) :], w2, slice(0, N))
        picked_words = []
        for part in range(S // GATHER):
            words = sb("picked_words%d" % part, [P, GATHER], U32)
            entries = offsets[:, part * GATHER // LIST_ROWS : (part + 1) * GATHER // LIST_ROWS]
            nc.vector.tensor_copy(words[:], table_words[:].indirect(entries))
            picked_words.append(words)

        warm = psum.tile([P, GATHER], F32, name="out_acc", tag="out", bufs=1)
        for t in range(PACK):
            product(warm[:], w3_mx, slice(t * P, (t + 1) * P), picked_words[0][:], picked_scales[:, 0:GATHER])

        w1_mx = mx_tiles("w1", H)
        w1_dealt = [sb("w1_dealt%d" % u, [P, 2 * P * PACK], BF16) for u in range(2)]
        for u in range(2):
            deal(nc.scalar.copy, w1_dealt[u], w1_raw[0], 0, u)
        deal(nc.vector.tensor_copy, w1_dealt[0], w1_raw[1], HALF // PACK, 0)
        deal(nc.scalar.copy, w1_dealt[1], w1_raw[1], HALF // PACK, 1)
        for t in range(PACK):
            cols = slice(t * P, (t + 1) * P)
            at = (t % 2) * P * PACK
            quantise(w1_mx[0][:, cols], w1_mx[1][:, cols], w1_dealt[t // 2][:, at : at + P * PACK])

        w2_mx = mx_tiles("w2", N)
        for step in range(first - LEAD_ROUND, CHUNKS + 1):
            if 0 <= step + 1 < CHUNKS:
                multiply_atoms(step + 1)
            if step + LEAD_ROUND < CHUNKS:
                round_edges(step + LEAD_ROUND)
            if first <= step + LEAD_QUANTISE < CHUNKS:
                quantise_edges(step + LEAD_QUANTISE)
            if first <= step + LEAD_FILTER < CHUNKS:
                filter_edges(step + LEAD_FILTER)
            if 0 <= step < CHUNKS:
                message(step)
            if step == OUT_GROUPS[0][-1]:
                w2_woven = weave(nc.scalar.copy, "w2_woven", w2_raw)
                quantise(w2_mx[0][:], w2_mx[1][:], w2_woven[:])
            if step >= 1 and group_of[step - 1][-1] == step - 1:
                project(group_of[step - 1])
